import numpy as np
import ml_dtypes


def mxq(x, axis, fmt="e4m3"):
    dtype, down = {"e4m3": (ml_dtypes.float8_e4m3fn, 7), "e5m2": (ml_dtypes.float8_e5m2, 14)}[fmt]
    v = np.moveaxis(np.asarray(x, np.float32).astype(ml_dtypes.bfloat16).astype(np.float64), axis, -1)
    blocks = v.reshape(v.shape[:-1] + (-1, 32))
    amax = np.abs(blocks).max(-1, keepdims=True)
    byte = np.maximum(np.where(amax > 0, np.frexp(amax)[1] - 1 + 127, 0) - down, 1)
    scale = np.exp2(byte - 127.0)
    codes = (blocks / scale).astype(np.float32).astype(dtype).astype(np.float64)
    return np.moveaxis((codes * scale).reshape(v.shape), -1, axis)


WIDE = False


def mx_kscale(k):
    if not WIDE:
        return np.ones(k)
    levels = np.array([10, -10, 5, -5, 0])
    if k % 512:
        return np.exp2(np.random.permutation(np.resize(levels, k // 32))).repeat(32)
    a = np.empty((k // 512, 16))
    for p in range(k // 512):
        a[p, :8] = np.random.permutation(np.resize(levels, 8))
        for g in range(8):
            far = levels[np.abs(levels - a[p, g]) >= 10]
            a[p, g + 8] = far[np.random.randint(len(far))]
    return np.exp2(a.ravel()).repeat(32)


BF16 = ml_dtypes.bfloat16


def bf(x):
    return np.asarray(x, np.float32).astype(BF16)


def f64(x):
    return np.asarray(x).astype(np.float64)

def planes(Y):
    n, m = Y.shape
    b = f64(bf(Y)).reshape(n // 32, 32, m)
    amax = np.abs(b).max(1)
    byte = np.clip(np.where(amax > 0, np.frexp(amax)[1] - 1 + 127 - 7, 1), 1, 254)
    codes = (b * np.exp2(127.0 - byte)[:, None, :]).reshape(n, m).astype(np.float32).astype(ml_dtypes.float8_e4m3fn).view(np.uint8)
    words = codes.reshape(n // 512, 128, 4, m).transpose(0, 1, 3, 2)
    return np.ascontiguousarray(words), np.ascontiguousarray(byte.astype(np.uint8).reshape(n // 512, 16, m))


T, L, F = 512, 2048, 1536

W_LOW, W_HIGH = 0.05, 3.09


def setup_inputs():
    s = mx_kscale(L)
    omega = np.random.uniform(W_LOW, W_HIGH, F)
    angle = np.arange(L)[:, None] * omega[None, :]
    unit = np.sqrt(2.0 / L)
    frames = np.random.randn(T, L) * s[None, :]
    cos_basis = unit * np.cos(angle) / s[:, None]
    sin_basis = unit * np.sin(angle) / s[:, None]
    magnitude = np.exp(0.8 * np.random.randn(F))
    phase = np.random.uniform(-np.pi, np.pi, F)
    return {
        "frames": bf(frames),
        "cos_basis": bf(cos_basis),
        "sin_basis": bf(sin_basis),
        "response_re": bf(magnitude * np.cos(phase)),
        "response_im": bf(magnitude * np.sin(phase)),
    }


def reference(frames, cos_basis, sin_basis, response_re, response_im):
    xq = mxq(f64(frames), 1, "e4m3")
    cq = mxq(f64(cos_basis), 0, "e4m3")
    sq = mxq(f64(sin_basis), 0, "e4m3")
    C = cq.T @ xq.T
    S = sq.T @ xq.T
    y = f64(response_re)[:, None] * C + f64(response_im)[:, None] * S
    Y = y
    words, scales = planes(Y)
    return y, words, scales

@@ -1,0 +1,232 @@
+from contextlib import ExitStack
+
+import concourse.mybir as mybir
+from concourse.masks import make_identity
+
+T, L, F = 512, 2048, 1536
+FLOPS = 2 * 2 * L * F * T
+
+F32 = mybir.dt.float32
+BF16 = mybir.dt.bfloat16
+U32 = mybir.dt.uint32
+I32 = mybir.dt.int32
+U8 = mybir.dt.uint8
+FP8X4 = mybir.dt.float8_e4m3fn_x4
+ALU = mybir.AluOpType
+COPY = mybir.ActivationFunctionType.Copy
+
+P = 128
+PACK = 4
+SPAN = P * PACK
+PASSES = L // SPAN
+GROUPS = F // SPAN
+STEPS = GROUPS * PASSES
+COS, SIN = 0, 1
+CAST_V = 256
+LAST_CAST_V = 176
+
+
+def tile_steered_fourier_spectrum_g2_kernel(
+    tc, frames, cos_basis, sin_basis, response_re, response_im, out_0, out_1, out_2
+):
+    nc = tc.nc
+    bases = (cos_basis, sin_basis)
+
+    with ExitStack() as ctx:
+        keep = ctx.enter_context(tc.tile_pool(name="keep", bufs=1))
+        work = ctx.enter_context(tc.tile_pool(name="work", bufs=1))
+        psum = ctx.enter_context(tc.psum_pool(name="psum", bufs=1))
+        ctx.enter_context(tc.manual_schedule())
+
+        raw = {}
+        frames_raw = {}
+        grouped = {}
+        codes = {}
+        turned = {}
+        sums = {}
+        frames_grouped = keep.tile([P, PASSES, T, 2], F32, align_bytes=64)
+        frames_codes = keep.tile([P, PASSES, T], U32, align_bytes=64)
+        frames_scales = keep.tile([P, PASSES, T], U8, align_bytes=64)
+        re_bf = keep.tile([P, GROUPS, PACK], BF16)
+        im_bf = keep.tile([P, GROUPS, PACK], BF16)
+        re_f32 = keep.tile([P, GROUPS, PACK], F32)
+        ident_bf = keep.tile([P, P], BF16)
+        ident = keep.tile([P, P], F32)
+        y = [keep.tile([P, PACK, T], F32, name="y%d" % g) for g in range(GROUPS)]
+        y_codes = [keep.tile([P, T], U32, name="y_codes%d" % g, align_bytes=64) for g in range(GROUPS)]
+        y_scales = [keep.tile([P, T], U8, name="y_scales%d" % g, align_bytes=64) for g in range(GROUPS)]
+        y_grouped = {}
+
+        def load_basis(b, s):
+            g, c = divmod(s, PASSES)
+            raw[b, s] = keep.tile([P, PACK, SPAN], BF16, name="raw%d_%d" % (b, s))
+            rows = bases[b][c * SPAN : (c + 1) * SPAN, g * SPAN : (g + 1) * SPAN]
+            nc.sync.dma_start(out=raw[b, s][:], in_=rows.rearrange("(p j) f -> p j f", j=PACK))
+
+        def load_frames(c):
+            frames_raw[c] = keep.tile([P, T // P, SPAN], BF16, name="frames_raw%d" % c)
+            cols = frames[:, c * SPAN : (c + 1) * SPAN]
+            nc.sync.dma_start(out=frames_raw[c][:], in_=cols.rearrange("(r p) k -> p r k", p=P))
+
+        def turn_frames(c):
+            words = frames_raw[c][:].bitcast(F32)
+            for h in range(2):
+                turned[c, h] = psum.tile([P, 2, 2, P], F32, name="bank%d" % (2 * c + h))
+                for r in range(2):
+                    for u in range(2):
+                        nc.tensor.transpose(turned[c, h][:, r, u, :], words[:, 2 * h + r, u : 2 * P : 2], ident[:])
+
+        def copy_on(engine):
+            return nc.vector.tensor_copy if engine == "V" else nc.scalar.copy
+
+        def group_frames(c, h, engine):
+            dst = frames_grouped[:, c, 2 * h * P : 2 * (h + 1) * P, :].rearrange("p (r m) u -> p r m u", r=2)
+            copy_on(engine)(out=dst, in_=turned[c, h][:].rearrange("p r u m -> p r m u"))
+
+        def quantize_frames(c):
+            nc.vector.quantize_mx(
+                out=frames_codes[:, c, :].bitcast(FP8X4),
+                scales=frames_scales[:, c, :],
+                in_=frames_grouped[:, c, :, :].rearrange("p m u -> p (m u)").bitcast(BF16),
+            )
+
+        def group_basis(b, s):
+            grouped[b, s] = work.tile([P, PACK, P, PACK], BF16, name="grouped%d" % b, bufs=3, align_bytes=64)
+            copy_on("V" if b == SIN else "S")(
+                out=grouped[b, s][:].rearrange("p t (n i) j -> p n t i j", i=2),
+                in_=raw[b, s][:].rearrange("p j (n i t) -> p n t i j", i=2, t=PACK),
+            )
+
+        def quantize_basis(b, s):
+            words = work.tile([P, SPAN], U32, name="words%d" % b, bufs=5, align_bytes=64)
+            scales = work.tile([P, SPAN], U8, name="scales%d" % b, bufs=5, align_bytes=64)
+            codes[b, s] = (words, scales)
+            nc.vector.quantize_mx(
+                out=words[:].bitcast(FP8X4), scales=scales[:], in_=grouped[b, s][:].rearrange("p t m j -> p (t m j)")
+            )
+
+        def multiply(b, s):
+            g, c = divmod(s, PASSES)
+            words, scales = codes[b, s]
+            for t in range(PACK):
+                if c == 0:
+                    sums[b, g, t] = psum.tile([P, T], F32, name="bank%d" % (PACK * b + t))
+                nc.tensor.matmul_mx(
+                    out=sums[b, g, t][:],
+                    lhsT=words[:, t * P : (t + 1) * P].bitcast(FP8X4),
+                    lhsT_scale=scales[:, t * P : (t + 1) * P],
+                    rhs=frames_codes[:, c, :].bitcast(FP8X4),
+                    rhs_scale=frames_scales[:, c, :],
+                    start=(c == 0),
+                    stop=(c == PASSES - 1),
+                )
+
+        def steer_cos(g):
+            for t in range(PACK):
+                nc.scalar.activation(out=y[g][:, t, :], in_=sums[COS, g, t][:], func=COPY, scale=re_f32[:, g, t : t + 1])
+
+        def steer_sin(g, lo, hi):
+            for t in range(PACK):
+                nc.vector.scalar_tensor_tensor(
+                    out=y[g][:, t, lo:hi],
+                    in0=sums[SIN, g, t][:, lo:hi],
+                    scalar=im_bf[:, g, t : t + 1],
+                    in1=y[g][:, t, lo:hi],
+                    op0=ALU.mult,
+                    op1=ALU.add,
+                )
+
+        def group_y(g, lo, hi, engine):
+            if g not in y_grouped:
+                y_grouped[g] = work.tile([P, T, PACK], BF16, name="y_grouped", bufs=2, align_bytes=64)
+            copy_on(engine)(out=y_grouped[g][:, lo:hi, :], in_=y[g][:, :, lo:hi].rearrange("p t m -> p m t"))
+
+        def quantize_y(g, lo, hi):
+            nc.vector.quantize_mx(
+                out=y_codes[g][:, lo:hi].bitcast(FP8X4),
+                scales=y_scales[g][:, lo:hi],
+                in_=y_grouped[g][:, lo:hi, :].rearrange("p m t -> p (m t)"),
+            )
+
+        def store_y(g, lo, hi):
+            rows = out_0[g * SPAN : (g + 1) * SPAN, lo:hi].rearrange("(p t) m -> p t m", t=PACK)
+            nc.sync.dma_start(out=rows, in_=y[g][:, :, lo:hi])
+
+        def store_words(g, lo, hi):
+            dst = out_1[g].rearrange("p m t -> p (m t)").bitcast(I32)
+            nc.sync.dma_start(out=dst[:, lo:hi], in_=y_codes[g][:, lo:hi].bitcast(I32))
+
+        def store_scales(g, queue):
+            for q in range(4):
+                queue.dma_start(
+                    out=out_2[g, 4 * q : 4 * q + 4, :].bitcast(I32), in_=y_scales[g][32 * q : 32 * q + 4, :].bitcast(I32)
+                )
+
+        load_basis(COS, 0)
+        load_basis(SIN, 0)
+        for c in range(PASSES):
+            load_frames(c)
+        for s in range(1, STEPS):
+            load_basis(COS, s)
+            load_basis(SIN, s)
+            if s == 1:
+                nc.sync.dma_start(out=re_bf[:], in_=response_re.rearrange("(g p t) -> p g t", p=P, t=PACK))
+                nc.sync.dma_start(out=im_bf[:], in_=response_im.rearrange("(g p t) -> p g t", p=P, t=PACK))
+
+        make_identity(nc, ident_bf[:])
+        nc.scalar.activation(out=ident[:], in_=ident_bf[:], func=COPY)
+
+        group_basis(COS, 0)
+        group_basis(SIN, 0)
+        quantize_basis(COS, 0)
+        quantize_basis(SIN, 0)
+        for c in range(PASSES):
+            turn_frames(c)
+        for c in range(PASSES - 1):
+            group_frames(c, 0, "S")
+            group_frames(c, 1, "S")
+            quantize_frames(c)
+        group_frames(PASSES - 1, 0, "V")
+        group_frames(PASSES - 1, 1, "V")
+        multiply(COS, 0)
+        multiply(SIN, 0)
+
+        for s in range(1, STEPS):
+            g, c = divmod(s, PASSES)
+            group_basis(COS, s)
+            group_basis(SIN, s)
+            if s == 1:
+                quantize_frames(PASSES - 1)
+            if s == 2:
+                nc.scalar.copy(out=re_f32[:], in_=re_bf[:])
+            if g > 0 and c == 1:
+                group_y(g - 1, 0, CAST_V, "V")
+                group_y(g - 1, CAST_V, T, "S")
+            quantize_basis(COS, s)
+            quantize_basis(SIN, s)
+            if g > 0 and c == 0:
+                steer_cos(g - 1)
+                steer_sin(g - 1, 0, T)
+                store_y(g - 1, 0, T)
+            if g > 0 and c == 1:
+                quantize_y(g - 1, 0, T)
+                store_words(g - 1, 0, T)
+                store_scales(g - 1, nc.sync)
+            multiply(COS, s)
+            multiply(SIN, s)
+
+        g = GROUPS - 1
+        half = T // 2
+        steer_cos(g)
+        steer_sin(g, 0, half)
+        store_y(g, 0, half)
+        group_y(g, 0, half, "S")
+        steer_sin(g, half, T)
+        store_y(g, half, T)
+        quantize_y(g, 0, half)
+        store_words(g, 0, half)
+        group_y(g, half, half + LAST_CAST_V, "V")
+        group_y(g, half + LAST_CAST_V, T, "S")
+        quantize_y(g, half, T)
+        store_words(g, half, T)
+        store_scales(g, nc.scalar)

@@ -47,9 +47,8 @@ def tile_steered_fourier_spectrum_g2_kernel(
         frames_grouped = keep.tile([P, PASSES, T, 2], F32, align_bytes=64)
         frames_codes = keep.tile([P, PASSES, T], U32, align_bytes=64)
         frames_scales = keep.tile([P, PASSES, T], U8, align_bytes=64)
-        re_bf = keep.tile([P, GROUPS, PACK], BF16)
-        im_bf = keep.tile([P, GROUPS, PACK], BF16)
-        re_f32 = keep.tile([P, GROUPS, PACK], F32)
+        response_rows = keep.tile([P, SPAN], BF16)
+        response = keep.tile([P, PACK, 2 * GROUPS], F32)
         ident_bf = keep.tile([P, P], BF16)
         ident = keep.tile([P, P], F32)
         y = [keep.tile([P, PACK, T], F32, name="y%d" % g) for g in range(GROUPS)]
@@ -92,18 +91,28 @@ def tile_steered_fourier_spectrum_g2_kernel(
 
         def group_basis(b, s):
             grouped[b, s] = work.tile([P, PACK, P, PACK], BF16, name="grouped%d" % b, bufs=3, align_bytes=64)
-            copy_on("V" if b == SIN else "S")(
-                out=grouped[b, s][:].rearrange("p t (n i) j -> p n t i j", i=2),
-                in_=raw[b, s][:].rearrange("p j (n i t) -> p n t i j", i=2, t=PACK),
+            dst = grouped[b, s][:].rearrange("p t (n i) j -> p n j t i", i=2)
+            src = raw[b, s][:].rearrange("p j (n i t) -> p n j t i", i=2, t=PACK)
+            for t in (0, 2):
+                copy_on("V" if b == SIN else "S")(out=dst[:, :, :, t : t + 2, :], in_=src[:, :, :, t : t + 2, :])
+
+        def quantize_basis(b, s, t0=0, t1=PACK):
+            if t0 == 0:
+                words = work.tile([P, SPAN], U32, name="words%d" % b, bufs=5, align_bytes=64)
+                scales = work.tile([P, SPAN], U8, name="scales%d" % b, bufs=5, align_bytes=64)
+                codes[b, s] = (words, scales)
+            words, scales = codes[b, s]
+            nc.vector.quantize_mx(
+                out=words[:, t0 * P : t1 * P].bitcast(FP8X4),
+                scales=scales[:, t0 * P : t1 * P],
+                in_=grouped[b, s][:, t0:t1, :, :].rearrange("p t m j -> p (t m j)"),
             )
 
-        def quantize_basis(b, s):
-            words = work.tile([P, SPAN], U32, name="words%d" % b, bufs=5, align_bytes=64)
-            scales = work.tile([P, SPAN], U8, name="scales%d" % b, bufs=5, align_bytes=64)
-            codes[b, s] = (words, scales)
-            nc.vector.quantize_mx(
-                out=words[:].bitcast(FP8X4), scales=scales[:], in_=grouped[b, s][:].rearrange("p t m j -> p (t m j)")
-            )
+        def turn_response():
+            bank = psum.tile([P, PACK, P], BF16, name="bank7")
+            for t in range(PACK):
+                nc.tensor.transpose(bank[:, t, :], response_rows[:, t:SPAN:PACK], ident_bf[:])
+            nc.scalar.copy(out=response[:], in_=bank[:, :, 0 : 2 * GROUPS])
 
         def multiply(b, s):
             g, c = divmod(s, PASSES)
@@ -123,14 +132,14 @@ def tile_steered_fourier_spectrum_g2_kernel(
 
         def steer_cos(g):
             for t in range(PACK):
-                nc.scalar.activation(out=y[g][:, t, :], in_=sums[COS, g, t][:], func=COPY, scale=re_f32[:, g, t : t + 1])
+                nc.scalar.activation(out=y[g][:, t, :], in_=sums[COS, g, t][:], func=COPY, scale=response[:, t, g : g + 1])
 
         def steer_sin(g, lo, hi):
             for t in range(PACK):
                 nc.vector.scalar_tensor_tensor(
                     out=y[g][:, t, lo:hi],
                     in0=sums[SIN, g, t][:, lo:hi],
-                    scalar=im_bf[:, g, t : t + 1],
+                    scalar=response[:, t, GROUPS + g : GROUPS + g + 1],
                     in1=y[g][:, t, lo:hi],
                     op0=ALU.mult,
                     op1=ALU.add,
@@ -139,7 +148,10 @@ def tile_steered_fourier_spectrum_g2_kernel(
         def group_y(g, lo, hi, engine):
             if g not in y_grouped:
                 y_grouped[g] = work.tile([P, T, PACK], BF16, name="y_grouped", bufs=2, align_bytes=64)
-            copy_on(engine)(out=y_grouped[g][:, lo:hi, :], in_=y[g][:, :, lo:hi].rearrange("p t m -> p m t"))
+            copy_on(engine)(
+                out=y_grouped[g][:, lo:hi, :].rearrange("p (n i) t -> p n t i", i=4),
+                in_=y[g][:, :, lo:hi].rearrange("p t (n i) -> p n t i", i=4),
+            )
 
         def quantize_y(g, lo, hi):
             nc.vector.quantize_mx(
@@ -162,16 +174,21 @@ def tile_steered_fourier_spectrum_g2_kernel(
                     out=out_2[g, 4 * q : 4 * q + 4, :].bitcast(I32), in_=y_scales[g][32 * q : 32 * q + 4, :].bitcast(I32)
                 )
 
+        nc.vector.memset(response_rows[:].bitcast(I32), 0)
+
         load_basis(COS, 0)
         load_basis(SIN, 0)
-        for c in range(PASSES):
-            load_frames(c)
-        for s in range(1, STEPS):
+        nc.sync.dma_start(out=response_rows[0:GROUPS, :], in_=response_re.rearrange("(g f) -> g f", g=GROUPS))
+        nc.sync.dma_start(out=response_rows[GROUPS : 2 * GROUPS, :], in_=response_im.rearrange("(g f) -> g f", g=GROUPS))
+        load_frames(0)
+        load_basis(COS, 1)
+        load_frames(1)
+        load_basis(SIN, 1)
+        load_frames(2)
+        load_frames(3)
+        for s in range(2, STEPS):
             load_basis(COS, s)
             load_basis(SIN, s)
-            if s == 1:
-                nc.sync.dma_start(out=re_bf[:], in_=response_re.rearrange("(g p t) -> p g t", p=P, t=PACK))
-                nc.sync.dma_start(out=im_bf[:], in_=response_im.rearrange("(g p t) -> p g t", p=P, t=PACK))
 
         make_identity(nc, ident_bf[:])
         nc.scalar.activation(out=ident[:], in_=ident_bf[:], func=COPY)
@@ -180,27 +197,39 @@ def tile_steered_fourier_spectrum_g2_kernel(
         group_basis(SIN, 0)
         quantize_basis(COS, 0)
         quantize_basis(SIN, 0)
-        for c in range(PASSES):
-            turn_frames(c)
-        for c in range(PASSES - 1):
-            group_frames(c, 0, "S")
-            group_frames(c, 1, "S")
-            quantize_frames(c)
-        group_frames(PASSES - 1, 0, "V")
-        group_frames(PASSES - 1, 1, "V")
-        multiply(COS, 0)
-        multiply(SIN, 0)
+        turn_frames(0)
+        group_frames(0, 0, "V")
+        group_frames(0, 1, "V")
+        quantize_frames(0)
+        group_basis(COS, 1)
+        group_basis(SIN, 1)
+        quantize_basis(COS, 1)
+        quantize_basis(SIN, 1)
+        turn_frames(1)
+        group_frames(1, 0, "S")
+        group_frames(1, 1, "S")
+        turn_response()
+        quantize_frames(1)
+        turn_frames(2)
+        group_frames(2, 0, "S")
+        group_frames(2, 1, "S")
+        turn_frames(3)
+        group_frames(3, 0, "S")
+        group_frames(3, 1, "V")
+        quantize_frames(2)
+        for s in range(2):
+            multiply(COS, s)
+            multiply(SIN, s)
 
-        for s in range(1, STEPS):
+        for s in range(2, STEPS - 1):
             g, c = divmod(s, PASSES)
             group_basis(COS, s)
             group_basis(SIN, s)
-            if s == 1:
-                quantize_frames(PASSES - 1)
             if s == 2:
-                nc.scalar.copy(out=re_f32[:], in_=re_bf[:])
+                quantize_frames(PASSES - 1)
             if g > 0 and c == 1:
                 group_y(g - 1, 0, CAST_V, "V")
+            if g == 1 and c == 1:
                 group_y(g - 1, CAST_V, T, "S")
             quantize_basis(COS, s)
             quantize_basis(SIN, s)
@@ -208,15 +237,27 @@ def tile_steered_fourier_spectrum_g2_kernel(
                 steer_cos(g - 1)
                 steer_sin(g - 1, 0, T)
                 store_y(g - 1, 0, T)
-            if g > 0 and c == 1:
+            if g == 1 and c == 1:
                 quantize_y(g - 1, 0, T)
                 store_words(g - 1, 0, T)
                 store_scales(g - 1, nc.sync)
             multiply(COS, s)
             multiply(SIN, s)
 
+        s = STEPS - 1
         g = GROUPS - 1
         half = T // 2
+        group_basis(COS, s)
+        quantize_basis(COS, s)
+        group_y(g - 1, CAST_V, T, "S")
+        group_basis(SIN, s)
+        quantize_basis(SIN, s, 0, 2)
+        quantize_basis(SIN, s, 2, PACK)
+        quantize_y(g - 1, 0, T)
+        store_words(g - 1, 0, T)
+        store_scales(g - 1, nc.sync)
+        multiply(COS, s)
+        multiply(SIN, s)
         steer_cos(g)
         steer_sin(g, 0, half)
         store_y(g, 0, half)

from contextlib import ExitStack

import concourse.mybir as mybir
from concourse.masks import make_identity

T, L, F = 512, 2048, 1536
FLOPS = 2 * 2 * L * F * T

F32 = mybir.dt.float32
BF16 = mybir.dt.bfloat16
U32 = mybir.dt.uint32
I32 = mybir.dt.int32
U8 = mybir.dt.uint8
FP8X4 = mybir.dt.float8_e4m3fn_x4
ALU = mybir.AluOpType
COPY = mybir.ActivationFunctionType.Copy

P = 128
PACK = 4
SPAN = P * PACK
PASSES = L // SPAN
GROUPS = F // SPAN
STEPS = GROUPS * PASSES
COS, SIN = 0, 1
CAST_V = 256
LAST_CAST_V = 176


def tile_steered_fourier_spectrum_g2_kernel(
    tc, frames, cos_basis, sin_basis, response_re, response_im, out_0, out_1, out_2
):
    nc = tc.nc
    bases = (cos_basis, sin_basis)

    with ExitStack() as ctx:
        keep = ctx.enter_context(tc.tile_pool(name="keep", bufs=1))
        work = ctx.enter_context(tc.tile_pool(name="work", bufs=1))
        psum = ctx.enter_context(tc.psum_pool(name="psum", bufs=1))
        ctx.enter_context(tc.manual_schedule())

        raw = {}
        frames_raw = {}
        grouped = {}
        codes = {}
        turned = {}
        sums = {}
        frames_grouped = keep.tile([P, PASSES, T, 2], F32, align_bytes=64)
        frames_codes = keep.tile([P, PASSES, T], U32, align_bytes=64)
        frames_scales = keep.tile([P, PASSES, T], U8, align_bytes=64)
        response_rows = keep.tile([P, SPAN], BF16)
        response = keep.tile([P, PACK, 2 * GROUPS], F32)
        ident_bf = keep.tile([P, P], BF16)
        ident = keep.tile([P, P], F32)
        y = [keep.tile([P, PACK, T], F32, name="y%d" % g) for g in range(GROUPS)]
        y_codes = [keep.tile([P, T], U32, name="y_codes%d" % g, align_bytes=64) for g in range(GROUPS)]
        y_scales = [keep.tile([P, T], U8, name="y_scales%d" % g, align_bytes=64) for g in range(GROUPS)]
        y_grouped = {}

        def load_basis(b, s):
            g, c = divmod(s, PASSES)
            raw[b, s] = keep.tile([P, PACK, SPAN], BF16, name="raw%d_%d" % (b, s))
            rows = bases[b][c * SPAN : (c + 1) * SPAN, g * SPAN : (g + 1) * SPAN]
            nc.sync.dma_start(out=raw[b, s][:], in_=rows.rearrange("(p j) f -> p j f", j=PACK))

        def load_frames(c):
            frames_raw[c] = keep.tile([P, T // P, SPAN], BF16, name="frames_raw%d" % c)
            cols = frames[:, c * SPAN : (c + 1) * SPAN]
            nc.sync.dma_start(out=frames_raw[c][:], in_=cols.rearrange("(r p) k -> p r k", p=P))

        def turn_frames(c):
            words = frames_raw[c][:].bitcast(F32)
            for h in range(2):
                turned[c, h] = psum.tile([P, 2, 2, P], F32, name="bank%d" % (2 * c + h))
                for r in range(2):
                    for u in range(2):
                        nc.tensor.transpose(turned[c, h][:, r, u, :], words[:, 2 * h + r, u : 2 * P : 2], ident[:])

        def copy_on(engine):
            return nc.vector.tensor_copy if engine == "V" else nc.scalar.copy

        def group_frames(c, h, engine):
            dst = frames_grouped[:, c, 2 * h * P : 2 * (h + 1) * P, :].rearrange("p (r m) u -> p r m u", r=2)
            copy_on(engine)(out=dst, in_=turned[c, h][:].rearrange("p r u m -> p r m u"))

        def quantize_frames(c):
            nc.vector.quantize_mx(
                out=frames_codes[:, c, :].bitcast(FP8X4),
                scales=frames_scales[:, c, :],
                in_=frames_grouped[:, c, :, :].rearrange("p m u -> p (m u)").bitcast(BF16),
            )

        def group_basis(b, s):
            grouped[b, s] = work.tile([P, PACK, P, PACK], BF16, name="grouped%d" % b, bufs=3, align_bytes=64)
            dst = grouped[b, s][:].rearrange("p t (n i) j -> p n j t i", i=2)
            src = raw[b, s][:].rearrange("p j (n i t) -> p n j t i", i=2, t=PACK)
            for t in (0, 2):
                copy_on("V" if b == SIN else "S")(out=dst[:, :, :, t : t + 2, :], in_=src[:, :, :, t : t + 2, :])

        def quantize_basis(b, s, t0=0, t1=PACK):
            if t0 == 0:
                words = work.tile([P, SPAN], U32, name="words%d" % b, bufs=5, align_bytes=64)
                scales = work.tile([P, SPAN], U8, name="scales%d" % b, bufs=5, align_bytes=64)
                codes[b, s] = (words, scales)
            words, scales = codes[b, s]
            nc.vector.quantize_mx(
                out=words[:, t0 * P : t1 * P].bitcast(FP8X4),
                scales=scales[:, t0 * P : t1 * P],
                in_=grouped[b, s][:, t0:t1, :, :].rearrange("p t m j -> p (t m j)"),
            )

        def turn_response():
            bank = psum.tile([P, PACK, P], BF16, name="bank7")
            for t in range(PACK):
                nc.tensor.transpose(bank[:, t, :], response_rows[:, t:SPAN:PACK], ident_bf[:])
            nc.scalar.copy(out=response[:], in_=bank[:, :, 0 : 2 * GROUPS])

        def multiply(b, s):
            g, c = divmod(s, PASSES)
            words, scales = codes[b, s]
            for t in range(PACK):
                if c == 0:
                    sums[b, g, t] = psum.tile([P, T], F32, name="bank%d" % (PACK * b + t))
                nc.tensor.matmul_mx(
                    out=sums[b, g, t][:],
                    lhsT=words[:, t * P : (t + 1) * P].bitcast(FP8X4),
                    lhsT_scale=scales[:, t * P : (t + 1) * P],
                    rhs=frames_codes[:, c, :].bitcast(FP8X4),
                    rhs_scale=frames_scales[:, c, :],
                    start=(c == 0),
                    stop=(c == PASSES - 1),
                )

        def steer_cos(g):
            for t in range(PACK):
                nc.scalar.activation(out=y[g][:, t, :], in_=sums[COS, g, t][:], func=COPY, scale=response[:, t, g : g + 1])

        def steer_sin(g, lo, hi):
            for t in range(PACK):
                nc.vector.scalar_tensor_tensor(
                    out=y[g][:, t, lo:hi],
                    in0=sums[SIN, g, t][:, lo:hi],
                    scalar=response[:, t, GROUPS + g : GROUPS + g + 1],
                    in1=y[g][:, t, lo:hi],
                    op0=ALU.mult,
                    op1=ALU.add,
                )

        def group_y(g, lo, hi, engine):
            if g not in y_grouped:
                y_grouped[g] = work.tile([P, T, PACK], BF16, name="y_grouped", bufs=2, align_bytes=64)
            copy_on(engine)(
                out=y_grouped[g][:, lo:hi, :].rearrange("p (n i) t -> p n t i", i=4),
                in_=y[g][:, :, lo:hi].rearrange("p t (n i) -> p n t i", i=4),
            )

        def quantize_y(g, lo, hi):
            nc.vector.quantize_mx(
                out=y_codes[g][:, lo:hi].bitcast(FP8X4),
                scales=y_scales[g][:, lo:hi],
                in_=y_grouped[g][:, lo:hi, :].rearrange("p m t -> p (m t)"),
            )

        def store_y(g, lo, hi):
            rows = out_0[g * SPAN : (g + 1) * SPAN, lo:hi].rearrange("(p t) m -> p t m", t=PACK)
            nc.sync.dma_start(out=rows, in_=y[g][:, :, lo:hi])

        def store_words(g, lo, hi):
            dst = out_1[g].rearrange("p m t -> p (m t)").bitcast(I32)
            nc.sync.dma_start(out=dst[:, lo:hi], in_=y_codes[g][:, lo:hi].bitcast(I32))

        def store_scales(g, queue):
            for q in range(4):
                queue.dma_start(
                    out=out_2[g, 4 * q : 4 * q + 4, :].bitcast(I32), in_=y_scales[g][32 * q : 32 * q + 4, :].bitcast(I32)
                )

        nc.vector.memset(response_rows[:].bitcast(I32), 0)

        load_basis(COS, 0)
        load_basis(SIN, 0)
        nc.sync.dma_start(out=response_rows[0:GROUPS, :], in_=response_re.rearrange("(g f) -> g f", g=GROUPS))
        nc.sync.dma_start(out=response_rows[GROUPS : 2 * GROUPS, :], in_=response_im.rearrange("(g f) -> g f", g=GROUPS))
        load_frames(0)
        load_basis(COS, 1)
        load_frames(1)
        load_basis(SIN, 1)
        load_frames(2)
        load_frames(3)
        for s in range(2, STEPS):
            load_basis(COS, s)
            load_basis(SIN, s)

        make_identity(nc, ident_bf[:])
        nc.scalar.activation(out=ident[:], in_=ident_bf[:], func=COPY)

        group_basis(COS, 0)
        group_basis(SIN, 0)
        quantize_basis(COS, 0)
        quantize_basis(SIN, 0)
        turn_frames(0)
        group_frames(0, 0, "V")
        group_frames(0, 1, "V")
        quantize_frames(0)
        group_basis(COS, 1)
        group_basis(SIN, 1)
        quantize_basis(COS, 1)
        quantize_basis(SIN, 1)
        turn_frames(1)
        group_frames(1, 0, "S")
        group_frames(1, 1, "S")
        turn_response()
        quantize_frames(1)
        turn_frames(2)
        group_frames(2, 0, "S")
        group_frames(2, 1, "S")
        turn_frames(3)
        group_frames(3, 0, "S")
        group_frames(3, 1, "V")
        quantize_frames(2)
        for s in range(2):
            multiply(COS, s)
            multiply(SIN, s)

        for s in range(2, STEPS - 1):
            g, c = divmod(s, PASSES)
            group_basis(COS, s)
            group_basis(SIN, s)
            if s == 2:
                quantize_frames(PASSES - 1)
            if g > 0 and c == 1:
                group_y(g - 1, 0, CAST_V, "V")
            if g == 1 and c == 1:
                group_y(g - 1, CAST_V, T, "S")
            quantize_basis(COS, s)
            quantize_basis(SIN, s)
            if g > 0 and c == 0:
                steer_cos(g - 1)
                steer_sin(g - 1, 0, T)
                store_y(g - 1, 0, T)
            if g == 1 and c == 1:
                quantize_y(g - 1, 0, T)
                store_words(g - 1, 0, T)
                store_scales(g - 1, nc.sync)
            multiply(COS, s)
            multiply(SIN, s)

        s = STEPS - 1
        g = GROUPS - 1
        half = T // 2
        group_basis(COS, s)
        quantize_basis(COS, s)
        group_y(g - 1, CAST_V, T, "S")
        group_basis(SIN, s)
        quantize_basis(SIN, s, 0, 2)
        quantize_basis(SIN, s, 2, PACK)
        quantize_y(g - 1, 0, T)
        store_words(g - 1, 0, T)
        store_scales(g - 1, nc.sync)
        multiply(COS, s)
        multiply(SIN, s)
        steer_cos(g)
        steer_sin(g, 0, half)
        store_y(g, 0, half)
        group_y(g, 0, half, "S")
        steer_sin(g, half, T)
        store_y(g, half, T)
        quantize_y(g, 0, half)
        store_words(g, 0, half)
        group_y(g, half, half + LAST_CAST_V, "V")
        group_y(g, half + LAST_CAST_V, T, "S")
        quantize_y(g, half, T)
        store_words(g, half, T)
        store_scales(g, nc.scalar)
